import numpy as np
import ml_dtypes


def mxq(x, axis, fmt="e4m3"):
    dtype, down = {"e4m3": (ml_dtypes.float8_e4m3fn, 7), "e5m2": (ml_dtypes.float8_e5m2, 14)}[fmt]
    v = np.moveaxis(np.asarray(x, np.float32).astype(ml_dtypes.bfloat16).astype(np.float64), axis, -1)
    blocks = v.reshape(v.shape[:-1] + (-1, 32))
    amax = np.abs(blocks).max(-1, keepdims=True)
    byte = np.maximum(np.where(amax > 0, np.frexp(amax)[1] - 1 + 127, 0) - down, 1)
    scale = np.exp2(byte - 127.0)
    codes = (blocks / scale).astype(np.float32).astype(dtype).astype(np.float64)
    return np.moveaxis((codes * scale).reshape(v.shape), -1, axis)


WIDE = False


def mx_kscale(k):
    if not WIDE:
        return np.ones(k)
    levels = np.array([10, -10, 5, -5, 0])
    if k % 512:
        return np.exp2(np.random.permutation(np.resize(levels, k // 32))).repeat(32)
    a = np.empty((k // 512, 16))
    for p in range(k // 512):
        a[p, :8] = np.random.permutation(np.resize(levels, 8))
        for g in range(8):
            far = levels[np.abs(levels - a[p, g]) >= 10]
            a[p, g + 8] = far[np.random.randint(len(far))]
    return np.exp2(a.ravel()).repeat(32)


def f64(x):
    return np.asarray(x).astype(np.float64)


def striped(idx):
    return np.tile(idx.reshape(-1, 16).T, (8, 1)).astype(np.uint16)


def unstriped(offs):
    return offs[:16].T.reshape(-1).astype(np.int64)


def pack_weight(w):
    k, n = w.shape
    w = f64(np.asarray(w, np.float32).astype(ml_dtypes.bfloat16)).reshape(k // 32, 32, n)
    amax = np.abs(w).max(1)
    byte = np.clip(np.where(amax > 0, np.frexp(amax)[1] - 1 + 127 - 7, 1), 1, 254)
    scaled = (w * np.exp2(127.0 - byte)[:, None, :]).reshape(k, n).astype(np.float32)
    words = np.ascontiguousarray(scaled.reshape(k // 512, 128, 4, n).transpose(0, 1, 3, 2)).astype(ml_dtypes.float8_e4m3fn).view(np.uint8)
    return words, np.ascontiguousarray(byte.astype(np.uint8).reshape(k // 512, 16, n))


def unpack_weight(words, scales):
    g, p, n, _ = words.shape
    vals = np.ascontiguousarray(words).view(ml_dtypes.float8_e4m3fn).astype(np.float64) * np.repeat(np.exp2(scales.astype(np.float64) - 127.0), 8, axis=1)[..., None]
    return vals.transpose(0, 1, 3, 2).reshape(g * 512, n)


K, T, S, N = 512, 1024, 512, 256


def setup_inputs():
    n = np.random.standard_normal
    s = mx_kscale(K)[:, None]
    packed_w1 = pack_weight(n((K, N)) / np.sqrt(K) / s)
    return {
        "xT": (n((K, T)) * s).astype(np.float32),
        "w1_words": packed_w1[0],
        "w1_scales": packed_w1[1],
        "offs": striped(np.random.permutation(T)[:S]),
    }


def reference(xT, w1_words, w1_scales, offs):
    xq = mxq(f64(xT)[:, unstriped(offs)], 0, "e4m3")
    y = unpack_weight(w1_words, w1_scales).T @ xq
    e = np.exp(y - y.max(axis=1, keepdims=True))
    return e / e.sum(axis=1, keepdims=True)

@@ -1,0 +1,129 @@
+from contextlib import ExitStack
+
+import concourse.mybir as mybir
+
+K, T, S, N = 512, 1024, 512, 256
+FLOPS = 2 * K * S * N
+
+F32 = mybir.dt.float32
+BF16 = mybir.dt.bfloat16
+I32 = mybir.dt.int32
+U32 = mybir.dt.uint32
+U16 = mybir.dt.uint16
+U8 = mybir.dt.uint8
+FP8X4 = mybir.dt.float8_e4m3fn_x4
+ACT = mybir.ActivationFunctionType
+ALU = mybir.AluOpType
+AX = mybir.AxisListType
+
+P = 128
+PACK = 4
+HALVES = 2
+H = S // HALVES
+SHARE = 128
+
+
+def tile_picked_rank_none_e_kernel(tc, xT, w1_words, w1_scales, offs, out):
+    nc = tc.nc
+    with ExitStack() as ctx:
+        keep = ctx.enter_context(tc.tile_pool(name="keep", bufs=1))
+        psum = ctx.enter_context(tc.psum_pool(name="psum", bufs=1))
+
+        offsets = keep.tile([P, S // 16], U16, name="offsets")
+        raw = [keep.tile([P, T], F32, name="raw%d" % t) for t in range(PACK)]
+        cast = [keep.tile([P, T], BF16, name="cast%d" % t) for t in range(2)]
+        w_codes = keep.tile([P, N], U32, name="w_codes", align_bytes=64)
+        w_scales = keep.tile([P, N], U8, name="w_scales", align_bytes=64)
+        grouped = [keep.tile([P, H, PACK], BF16, name="grouped%d" % h, align_bytes=64) for h in range(HALVES)]
+        x_codes = [keep.tile([P, H], U32, name="x_codes%d" % h, align_bytes=64) for h in range(HALVES)]
+        x_scales = [keep.tile([P, H], U8, name="x_scales%d" % h, align_bytes=64) for h in range(HALVES)]
+
+        planes = xT.rearrange("(p t) c -> p t c", t=PACK)
+        nc.vector.memset(w_scales[:].bitcast(I32), 0)
+        warm_in = keep.tile([P, 1], F32, name="warm_in")
+        warm_out = keep.tile([P, 1], F32, name="warm_out")
+        nc.vector.memset(warm_in[:], 0.0)
+        nc.scalar.activation(warm_out[:], warm_in[:], ACT.Exp)
+        nc.sync.dma_start(out=raw[0][:], in_=planes[:, 0, :])
+        nc.sync.dma_start(offsets[:], offs)
+        for t in (2, 1, 3):
+            nc.sync.dma_start(out=raw[t][:], in_=planes[:, t, :])
+        nc.sync.dma_start(out=w_codes[:].bitcast(I32), in_=w1_words[0].rearrange("p n r -> p (n r)").bitcast(I32))
+        for q in range(4):
+            nc.sync.dma_start(
+                out=w_scales[32 * q : 32 * q + 4, :].bitcast(I32),
+                in_=w1_scales[0, 4 * q : 4 * q + 4, :].bitcast(I32),
+            )
+
+        def gather(engine, t, lo, hi):
+            h = lo // H
+            target = grouped[h][:, lo - h * H : hi - h * H, t]
+            picks = offsets[:, lo // 16 : hi // 16]
+            if engine == "scalar":
+                nc.scalar.activation(target, cast[t][:].indirect(picks), ACT.Copy)
+            else:
+                nc.vector.tensor_copy(target, raw[t][:].indirect(picks))
+
+        nc.vector.tensor_copy(cast[0][:], raw[0][:])
+        gather("vector", 0, 0, SHARE)
+        gather("scalar", 0, SHARE, H)
+        gather("scalar", 0, H, S)
+        gather("vector", 2, 0, H)
+        gather("vector", 2, H, S)
+        nc.scalar.copy(cast[1][:], raw[1][:])
+        gather("vector", 1, 0, SHARE)
+        gather("scalar", 1, SHARE, H)
+        gather("scalar", 1, H, S)
+        gather("vector", 3, 0, H)
+        gather("vector", 3, H, S)
+
+        for h in range(HALVES):
+            nc.vector.quantize_mx(
+                out=x_codes[h][:].bitcast(FP8X4),
+                scales=x_scales[h][:],
+                in_=grouped[h][:].rearrange("p c t -> p (c t)"),
+            )
+
+        def multiply(target, b, h):
+            nc.tensor.matmul_mx(
+                out=target,
+                lhsT=w_codes[:, b * P : (b + 1) * P].bitcast(FP8X4),
+                lhsT_scale=w_scales[:, b * P : (b + 1) * P],
+                rhs=x_codes[h][:].bitcast(FP8X4),
+                rhs_scale=x_scales[h][:],
+                start=True,
+                stop=True,
+            )
+
+        first = [psum.tile([P, H], F32, name="first%d" % h) for h in range(HALVES)]
+        second = psum.tile([P, S], F32, name="second")
+        for h in range(HALVES):
+            multiply(first[h][:], 0, h)
+        for h in range(HALVES):
+            multiply(second[:, h * H : (h + 1) * H], 1, h)
+
+        neg_max = [keep.tile([P, 1], F32, name="neg_max%d" % b) for b in range(2)]
+        total = [keep.tile([P, 1], F32, name="total%d" % b) for b in range(2)]
+        inverse = [keep.tile([P, 1], F32, name="inverse%d" % b) for b in range(2)]
+        e = [keep.tile([P, S], F32, name="e%d" % b) for b in range(2)]
+
+        negated = keep.tile([P, S], F32, name="negated")
+        running = neg_max[1]
+        nc.vector.tensor_scalar(negated[:, :H], first[0][:], -1.0, None, ALU.mult, ALU.min, accum_out=running[:])
+        nc.vector.tensor_scalar(negated[:, H:], first[1][:], -1.0, running[:], ALU.mult, ALU.min, accum_out=neg_max[0][:])
+        nc.scalar.activation(e[0][:], negated[:], ACT.Exp, bias=neg_max[0][:], scale=-1.0, accum_out=total[0][:])
+        nc.vector.tensor_reduce(neg_max[1][:], second[:], AX.X, ALU.max, negate=True)
+        nc.scalar.activation(e[1][:], second[:], ACT.Exp, bias=neg_max[1][:], scale=1.0, accum_out=total[1][:])
+
+        result = keep.tile([P, S], F32, name="result")
+        nc.vector.reciprocal(inverse[0][:], total[0][:])
+        nc.vector.tensor_scalar(result[:], e[0][:], inverse[0][:], None, ALU.mult)
+        nc.sync.dma_start(out=out[:P, :], in_=result[:])
+
+        left = keep.tile([P, H], F32, name="left")
+        right = keep.tile([P, H], F32, name="right")
+        nc.vector.reciprocal(inverse[1][:], total[1][:])
+        nc.vector.tensor_scalar(left[:], e[1][:, :H], inverse[1][:], None, ALU.mult)
+        nc.sync.dma_start(out=out[P:, :H], in_=left[:])
+        nc.scalar.activation(right[:], e[1][:, H:], ACT.Copy, scale=inverse[1][:])
+        nc.scalar.dma_start(out=out[P:, H:], in_=right[:])

@@ -84,46 +84,37 @@ def tile_picked_rank_none_e_kernel(tc, xT, w1_words, w1_scales, offs, out):
                 in_=grouped[h][:].rearrange("p c t -> p (c t)"),
             )
 
-        def multiply(target, b, h):
-            nc.tensor.matmul_mx(
-                out=target,
-                lhsT=w_codes[:, b * P : (b + 1) * P].bitcast(FP8X4),
-                lhsT_scale=w_scales[:, b * P : (b + 1) * P],
-                rhs=x_codes[h][:].bitcast(FP8X4),
-                rhs_scale=x_scales[h][:],
-                start=True,
-                stop=True,
-            )
+        blocks = N // P
+        scores = [psum.tile([P, S], F32, name="scores%d" % b) for b in range(blocks)]
+        for b in range(blocks):
+            for h in range(HALVES):
+                nc.tensor.matmul_mx(
+                    out=scores[b][:, h * H : (h + 1) * H],
+                    lhsT=w_codes[:, b * P : (b + 1) * P].bitcast(FP8X4),
+                    lhsT_scale=w_scales[:, b * P : (b + 1) * P],
+                    rhs=x_codes[h][:].bitcast(FP8X4),
+                    rhs_scale=x_scales[h][:],
+                    start=True,
+                    stop=True,
+                )
 
-        first = [psum.tile([P, H], F32, name="first%d" % h) for h in range(HALVES)]
-        second = psum.tile([P, S], F32, name="second")
-        for h in range(HALVES):
-            multiply(first[h][:], 0, h)
-        for h in range(HALVES):
-            multiply(second[:, h * H : (h + 1) * H], 1, h)
-
-        neg_max = [keep.tile([P, 1], F32, name="neg_max%d" % b) for b in range(2)]
-        total = [keep.tile([P, 1], F32, name="total%d" % b) for b in range(2)]
-        inverse = [keep.tile([P, 1], F32, name="inverse%d" % b) for b in range(2)]
-        e = [keep.tile([P, S], F32, name="e%d" % b) for b in range(2)]
-
-        negated = keep.tile([P, S], F32, name="negated")
-        running = neg_max[1]
-        nc.vector.tensor_scalar(negated[:, :H], first[0][:], -1.0, None, ALU.mult, ALU.min, accum_out=running[:])
-        nc.vector.tensor_scalar(negated[:, H:], first[1][:], -1.0, running[:], ALU.mult, ALU.min, accum_out=neg_max[0][:])
-        nc.scalar.activation(e[0][:], negated[:], ACT.Exp, bias=neg_max[0][:], scale=-1.0, accum_out=total[0][:])
-        nc.vector.tensor_reduce(neg_max[1][:], second[:], AX.X, ALU.max, negate=True)
-        nc.scalar.activation(e[1][:], second[:], ACT.Exp, bias=neg_max[1][:], scale=1.0, accum_out=total[1][:])
-
-        result = keep.tile([P, S], F32, name="result")
-        nc.vector.reciprocal(inverse[0][:], total[0][:])
-        nc.vector.tensor_scalar(result[:], e[0][:], inverse[0][:], None, ALU.mult)
-        nc.sync.dma_start(out=out[:P, :], in_=result[:])
-
-        left = keep.tile([P, H], F32, name="left")
-        right = keep.tile([P, H], F32, name="right")
-        nc.vector.reciprocal(inverse[1][:], total[1][:])
-        nc.vector.tensor_scalar(left[:], e[1][:, :H], inverse[1][:], None, ALU.mult)
-        nc.sync.dma_start(out=out[P:, :H], in_=left[:])
-        nc.scalar.activation(right[:], e[1][:, H:], ACT.Copy, scale=inverse[1][:])
-        nc.scalar.dma_start(out=out[P:, H:], in_=right[:])
+        for b in range(blocks):
+            neg_max = keep.tile([P, 1], F32, name="neg_max%d" % b)
+            total = keep.tile([P, 1], F32, name="total%d" % b)
+            inverse = keep.tile([P, 1], F32, name="inverse%d" % b)
+            e = keep.tile([P, S], F32, name="e%d" % b)
+            nc.vector.tensor_reduce(neg_max[:], scores[b][:], AX.X, ALU.max, negate=True)
+            nc.scalar.activation(e[:], scores[b][:], ACT.Exp, bias=neg_max[:], scale=1.0, accum_out=total[:])
+            nc.vector.reciprocal(inverse[:], total[:])
+            rows = out[b * P : (b + 1) * P, :]
+            if b < blocks - 1:
+                result = keep.tile([P, S], F32, name="result")
+                nc.vector.tensor_scalar(result[:], e[:], inverse[:], None, ALU.mult)
+                nc.sync.dma_start(out=rows, in_=result[:])
+            else:
+                left = keep.tile([P, H], F32, name="left")
+                right = keep.tile([P, H], F32, name="right")
+                nc.vector.tensor_scalar(left[:], e[:, :H], inverse[:], None, ALU.mult)
+                nc.sync.dma_start(out=rows[:, :H], in_=left[:])
+                nc.scalar.activation(right[:], e[:, H:], ACT.Copy, scale=inverse[:])
+                nc.scalar.dma_start(out=rows[:, H:], in_=right[:])

@@ -35,8 +35,8 @@ def tile_picked_rank_none_e_kernel(tc, xT, w1_words, w1_scales, offs, out):
         w_codes = keep.tile([P, N], U32, name="w_codes", align_bytes=64)
         w_scales = keep.tile([P, N], U8, name="w_scales", align_bytes=64)
         grouped = [keep.tile([P, H, PACK], BF16, name="grouped%d" % h, align_bytes=64) for h in range(HALVES)]
-        x_codes = [keep.tile([P, H], U32, name="x_codes%d" % h, align_bytes=64) for h in range(HALVES)]
-        x_scales = [keep.tile([P, H], U8, name="x_scales%d" % h, align_bytes=64) for h in range(HALVES)]
+        x_codes = keep.tile([P, S], U32, name="x_codes", align_bytes=64)
+        x_scales = keep.tile([P, S], U8, name="x_scales", align_bytes=64)
 
         planes = xT.rearrange("(p t) c -> p t c", t=PACK)
         nc.vector.memset(w_scales[:].bitcast(I32), 0)
@@ -79,21 +79,23 @@ def tile_picked_rank_none_e_kernel(tc, xT, w1_words, w1_scales, offs, out):
 
         for h in range(HALVES):
             nc.vector.quantize_mx(
-                out=x_codes[h][:].bitcast(FP8X4),
-                scales=x_scales[h][:],
+                out=x_codes[:, h * H : (h + 1) * H].bitcast(FP8X4),
+                scales=x_scales[:, h * H : (h + 1) * H],
                 in_=grouped[h][:].rearrange("p c t -> p (c t)"),
             )
 
         blocks = N // P
         scores = [psum.tile([P, S], F32, name="scores%d" % b) for b in range(blocks)]
         for b in range(blocks):
-            for h in range(HALVES):
+            width = H if b == 0 else S
+            for lo in range(0, S, width):
+                cols = slice(lo, lo + width)
                 nc.tensor.matmul_mx(
-                    out=scores[b][:, h * H : (h + 1) * H],
+                    out=scores[b][:, cols],
                     lhsT=w_codes[:, b * P : (b + 1) * P].bitcast(FP8X4),
                     lhsT_scale=w_scales[:, b * P : (b + 1) * P],
-                    rhs=x_codes[h][:].bitcast(FP8X4),
-                    rhs_scale=x_scales[h][:],
+                    rhs=x_codes[:, cols].bitcast(FP8X4),
+                    rhs_scale=x_scales[:, cols],
                     start=True,
                     stop=True,
                 )
@@ -106,15 +108,6 @@ def tile_picked_rank_none_e_kernel(tc, xT, w1_words, w1_scales, offs, out):
             nc.vector.tensor_reduce(neg_max[:], scores[b][:], AX.X, ALU.max, negate=True)
             nc.scalar.activation(e[:], scores[b][:], ACT.Exp, bias=neg_max[:], scale=1.0, accum_out=total[:])
             nc.vector.reciprocal(inverse[:], total[:])
-            rows = out[b * P : (b + 1) * P, :]
-            if b < blocks - 1:
-                result = keep.tile([P, S], F32, name="result")
-                nc.vector.tensor_scalar(result[:], e[:], inverse[:], None, ALU.mult)
-                nc.sync.dma_start(out=rows, in_=result[:])
-            else:
-                left = keep.tile([P, H], F32, name="left")
-                right = keep.tile([P, H], F32, name="right")
-                nc.vector.tensor_scalar(left[:], e[:, :H], inverse[:], None, ALU.mult)
-                nc.sync.dma_start(out=rows[:, :H], in_=left[:])
-                nc.scalar.activation(right[:], e[:, H:], ACT.Copy, scale=inverse[:])
-                nc.scalar.dma_start(out=rows[:, H:], in_=right[:])
+            result = keep.tile([P, S], F32, name="result%d" % b)
+            nc.vector.tensor_scalar(result[:], e[:], inverse[:], None, ALU.mult)
+            nc.sync.dma_start(out=out[b * P : (b + 1) * P, :], in_=result[:])

@@ -50,7 +50,7 @@ def tile_picked_rank_none_e_kernel(tc, xT, w1_words, w1_scales, offs, out):
             nc.sync.dma_start(out=raw[t][:], in_=planes[:, t, :])
         nc.sync.dma_start(out=w_codes[:].bitcast(I32), in_=w1_words[0].rearrange("p n r -> p (n r)").bitcast(I32))
         for q in range(4):
-            nc.sync.dma_start(
+            nc.scalar.dma_start(
                 out=w_scales[32 * q : 32 * q + 4, :].bitcast(I32),
                 in_=w1_scales[0, 4 * q : 4 * q + 4, :].bitcast(I32),
             )

@@ -21,6 +21,7 @@ PACK = 4
 HALVES = 2
 H = S // HALVES
 SHARE = 128
+Q = 128
 
 
 def tile_picked_rank_none_e_kernel(tc, xT, w1_words, w1_scales, offs, out):
@@ -77,17 +78,18 @@ def tile_picked_rank_none_e_kernel(tc, xT, w1_words, w1_scales, offs, out):
         gather("vector", 3, 0, H)
         gather("vector", 3, H, S)
 
-        for h in range(HALVES):
+        for lo in range(0, S, Q):
+            h = lo // H
             nc.vector.quantize_mx(
-                out=x_codes[:, h * H : (h + 1) * H].bitcast(FP8X4),
-                scales=x_scales[:, h * H : (h + 1) * H],
-                in_=grouped[h][:].rearrange("p c t -> p (c t)"),
+                out=x_codes[:, lo : lo + Q].bitcast(FP8X4),
+                scales=x_scales[:, lo : lo + Q],
+                in_=grouped[h][:, lo - h * H : lo - h * H + Q, :].rearrange("p c t -> p (c t)"),
             )
 
         blocks = N // P
         scores = [psum.tile([P, S], F32, name="scores%d" % b) for b in range(blocks)]
         for b in range(blocks):
-            width = H if b == 0 else S
+            width = Q if b == 0 else S
             for lo in range(0, S, width):
                 cols = slice(lo, lo + width)
                 nc.tensor.matmul_mx(

@@ -18,10 +18,10 @@ AX = mybir.AxisListType
 
 P = 128
 PACK = 4
-HALVES = 2
-H = S // HALVES
 SHARE = 128
 Q = 128
+PLACED = 192
+UNITS = ((384, 512), (320, 384), (192, 320), (0, 128), (128, 192))
 
 
 def tile_picked_rank_none_e_kernel(tc, xT, w1_words, w1_scales, offs, out):
@@ -33,9 +33,10 @@ def tile_picked_rank_none_e_kernel(tc, xT, w1_words, w1_scales, offs, out):
         offsets = keep.tile([P, S // 16], U16, name="offsets")
         raw = [keep.tile([P, T], F32, name="raw%d" % t) for t in range(PACK)]
         cast = [keep.tile([P, T], BF16, name="cast%d" % t) for t in range(2)]
+        picked = keep.tile([P, S], BF16, name="picked")
         w_codes = keep.tile([P, N], U32, name="w_codes", align_bytes=64)
         w_scales = keep.tile([P, N], U8, name="w_scales", align_bytes=64)
-        grouped = [keep.tile([P, H, PACK], BF16, name="grouped%d" % h, align_bytes=64) for h in range(HALVES)]
+        grouped = keep.tile([P, S, PACK], BF16, name="grouped", align_bytes=64)
         x_codes = keep.tile([P, S], U32, name="x_codes", align_bytes=64)
         x_scales = keep.tile([P, S], U8, name="x_scales", align_bytes=64)
 
@@ -56,42 +57,39 @@ def tile_picked_rank_none_e_kernel(tc, xT, w1_words, w1_scales, offs, out):
                 in_=w1_scales[0, 4 * q : 4 * q + 4, :].bitcast(I32),
             )
 
-        def gather(engine, t, lo, hi):
-            h = lo // H
-            target = grouped[h][:, lo - h * H : hi - h * H, t]
-            picks = offsets[:, lo // 16 : hi // 16]
-            if engine == "scalar":
-                nc.scalar.activation(target, cast[t][:].indirect(picks), ACT.Copy)
-            else:
-                nc.vector.tensor_copy(target, raw[t][:].indirect(picks))
+        def picks(lo, hi):
+            return offsets[:, lo // 16 : hi // 16]
 
-        nc.vector.tensor_copy(cast[0][:], raw[0][:])
-        gather("vector", 0, 0, SHARE)
-        gather("scalar", 0, SHARE, H)
-        gather("scalar", 0, H, S)
-        gather("vector", 2, 0, H)
-        gather("vector", 2, H, S)
-        nc.scalar.copy(cast[1][:], raw[1][:])
-        gather("vector", 1, 0, SHARE)
-        gather("scalar", 1, SHARE, H)
-        gather("scalar", 1, H, S)
-        gather("vector", 3, 0, H)
-        gather("vector", 3, H, S)
+        def share(t):
+            nc.vector.tensor_copy(cast[t][:], raw[t][:])
+            nc.vector.tensor_copy(grouped[:, :SHARE, t], raw[t][:].indirect(picks(0, SHARE)))
+            nc.scalar.activation(grouped[:, SHARE:, t], cast[t][:].indirect(picks(SHARE, S)), ACT.Copy)
 
-        for lo in range(0, S, Q):
-            h = lo // H
+        share(0)
+        nc.vector.tensor_copy(picked[:, PLACED:], raw[2][:].indirect(picks(PLACED, S)))
+        nc.vector.tensor_copy(picked[:, :PLACED], raw[2][:].indirect(picks(0, PLACED)))
+        nc.scalar.copy(grouped[:, PLACED:, 2], picked[:, PLACED:])
+        share(1)
+
+        nc.vector.tensor_copy(picked[:, PLACED : 2 * PLACED], raw[3][:].indirect(picks(0, PLACED)))
+        pairs = picked[:, : 2 * PLACED].rearrange("p (u c) -> p c u", u=2)
+        for lo, hi in ((0, Q), (Q, PLACED)):
+            nc.scalar.copy(grouped[:, lo:hi, 2:4], pairs[:, lo:hi, :])
+        for lo, hi in ((PLACED + Q, S), (PLACED, PLACED + Q)):
+            nc.vector.tensor_copy(grouped[:, lo:hi, 3], raw[3][:].indirect(picks(lo, hi)))
+
+        for lo, hi in UNITS:
             nc.vector.quantize_mx(
-                out=x_codes[:, lo : lo + Q].bitcast(FP8X4),
-                scales=x_scales[:, lo : lo + Q],
-                in_=grouped[h][:, lo - h * H : lo - h * H + Q, :].rearrange("p c t -> p (c t)"),
+                out=x_codes[:, lo:hi].bitcast(FP8X4),
+                scales=x_scales[:, lo:hi],
+                in_=grouped[:, lo:hi, :].rearrange("p c t -> p (c t)"),
             )
 
         blocks = N // P
         scores = [psum.tile([P, S], F32, name="scores%d" % b) for b in range(blocks)]
         for b in range(blocks):
-            width = Q if b == 0 else S
-            for lo in range(0, S, width):
-                cols = slice(lo, lo + width)
+            for lo, hi in UNITS if b == 0 else ((0, S),):
+                cols = slice(lo, hi)
                 nc.tensor.matmul_mx(
                     out=scores[b][:, cols],
                     lhsT=w_codes[:, b * P : (b + 1) * P].bitcast(FP8X4),

@@ -33,7 +33,7 @@ def tile_picked_rank_none_e_kernel(tc, xT, w1_words, w1_scales, offs, out):
         offsets = keep.tile([P, S // 16], U16, name="offsets")
         raw = [keep.tile([P, T], F32, name="raw%d" % t) for t in range(PACK)]
         cast = [keep.tile([P, T], BF16, name="cast%d" % t) for t in range(2)]
-        picked = keep.tile([P, S], BF16, name="picked")
+        picked = keep.tile([P, S + Q], BF16, name="picked")
         w_codes = keep.tile([P, N], U32, name="w_codes", align_bytes=64)
         w_scales = keep.tile([P, N], U8, name="w_scales", align_bytes=64)
         grouped = keep.tile([P, S, PACK], BF16, name="grouped", align_bytes=64)
@@ -66,14 +66,14 @@ def tile_picked_rank_none_e_kernel(tc, xT, w1_words, w1_scales, offs, out):
             nc.scalar.activation(grouped[:, SHARE:, t], cast[t][:].indirect(picks(SHARE, S)), ACT.Copy)
 
         share(0)
-        nc.vector.tensor_copy(picked[:, PLACED:], raw[2][:].indirect(picks(PLACED, S)))
+        nc.vector.tensor_copy(picked[:, PLACED + Q :], raw[2][:].indirect(picks(PLACED, S)))
         nc.vector.tensor_copy(picked[:, :PLACED], raw[2][:].indirect(picks(0, PLACED)))
-        nc.scalar.copy(grouped[:, PLACED:, 2], picked[:, PLACED:])
+        nc.scalar.copy(grouped[:, PLACED:, 2], picked[:, PLACED + Q :])
         share(1)
 
-        nc.vector.tensor_copy(picked[:, PLACED : 2 * PLACED], raw[3][:].indirect(picks(0, PLACED)))
         pairs = picked[:, : 2 * PLACED].rearrange("p (u c) -> p c u", u=2)
         for lo, hi in ((0, Q), (Q, PLACED)):
+            nc.vector.tensor_copy(picked[:, PLACED + lo : PLACED + hi], raw[3][:].indirect(picks(lo, hi)))
             nc.scalar.copy(grouped[:, lo:hi, 2:4], pairs[:, lo:hi, :])
         for lo, hi in ((PLACED + Q, S), (PLACED, PLACED + Q)):
             nc.vector.tensor_copy(grouped[:, lo:hi, 3], raw[3][:].indirect(picks(lo, hi)))

@@ -18,7 +18,7 @@ AX = mybir.AxisListType
 
 P = 128
 PACK = 4
-SHARE = 128
+SHARE = 160
 Q = 128
 PLACED = 192
 UNITS = ((384, 512), (320, 384), (192, 320), (0, 128), (128, 192))

@@ -18,10 +18,10 @@ AX = mybir.AxisListType
 
 P = 128
 PACK = 4
-SHARE = 160
+SHARE = 288
 Q = 128
-PLACED = 192
-UNITS = ((384, 512), (320, 384), (192, 320), (0, 128), (128, 192))
+PIECES = ((SHARE, 384), (384, 512))
+UNITS = ((0, 128), (128, 256), (256, 384), (384, 512))
 
 
 def tile_picked_rank_none_e_kernel(tc, xT, w1_words, w1_scales, offs, out):
@@ -32,8 +32,7 @@ def tile_picked_rank_none_e_kernel(tc, xT, w1_words, w1_scales, offs, out):
 
         offsets = keep.tile([P, S // 16], U16, name="offsets")
         raw = [keep.tile([P, T], F32, name="raw%d" % t) for t in range(PACK)]
-        cast = [keep.tile([P, T], BF16, name="cast%d" % t) for t in range(2)]
-        picked = keep.tile([P, S + Q], BF16, name="picked")
+        rows = keep.tile([P, PACK, S - SHARE], BF16, name="rows")
         w_codes = keep.tile([P, N], U32, name="w_codes", align_bytes=64)
         w_scales = keep.tile([P, N], U8, name="w_scales", align_bytes=64)
         grouped = keep.tile([P, S, PACK], BF16, name="grouped", align_bytes=64)
@@ -48,7 +47,7 @@ def tile_picked_rank_none_e_kernel(tc, xT, w1_words, w1_scales, offs, out):
         nc.scalar.activation(warm_out[:], warm_in[:], ACT.Exp)
         nc.sync.dma_start(out=raw[0][:], in_=planes[:, 0, :])
         nc.sync.dma_start(offsets[:], offs)
-        for t in (2, 1, 3):
+        for t in range(1, PACK):
             nc.sync.dma_start(out=raw[t][:], in_=planes[:, t, :])
         nc.sync.dma_start(out=w_codes[:].bitcast(I32), in_=w1_words[0].rearrange("p n r -> p (n r)").bitcast(I32))
         for q in range(4):
@@ -60,23 +59,28 @@ def tile_picked_rank_none_e_kernel(tc, xT, w1_words, w1_scales, offs, out):
         def picks(lo, hi):
             return offsets[:, lo // 16 : hi // 16]
 
-        def share(t):
-            nc.vector.tensor_copy(cast[t][:], raw[t][:])
-            nc.vector.tensor_copy(grouped[:, :SHARE, t], raw[t][:].indirect(picks(0, SHARE)))
-            nc.scalar.activation(grouped[:, SHARE:, t], cast[t][:].indirect(picks(SHARE, S)), ACT.Copy)
+        def direct(t, lo, hi):
+            nc.vector.tensor_copy(grouped[:, lo:hi, t], raw[t][:].indirect(picks(lo, hi)))
 
-        share(0)
-        nc.vector.tensor_copy(picked[:, PLACED + Q :], raw[2][:].indirect(picks(PLACED, S)))
-        nc.vector.tensor_copy(picked[:, :PLACED], raw[2][:].indirect(picks(0, PLACED)))
-        nc.scalar.copy(grouped[:, PLACED:, 2], picked[:, PLACED + Q :])
-        share(1)
+        def fetch(t, lo, hi):
+            nc.scalar.activation(rows[:, t, lo - SHARE : hi - SHARE], raw[t][:].indirect(picks(lo, hi)), ACT.Copy)
 
-        pairs = picked[:, : 2 * PLACED].rearrange("p (u c) -> p c u", u=2)
-        for lo, hi in ((0, Q), (Q, PLACED)):
-            nc.vector.tensor_copy(picked[:, PLACED + lo : PLACED + hi], raw[3][:].indirect(picks(lo, hi)))
-            nc.scalar.copy(grouped[:, lo:hi, 2:4], pairs[:, lo:hi, :])
-        for lo, hi in ((PLACED + Q, S), (PLACED, PLACED + Q)):
-            nc.vector.tensor_copy(grouped[:, lo:hi, 3], raw[3][:].indirect(picks(lo, hi)))
+        def place(t, lo, hi):
+            pair = rows[:, t : t + 2, lo - SHARE : hi - SHARE].rearrange("p u c -> p c u")
+            nc.scalar.copy(grouped[:, lo:hi, t : t + 2], pair)
+
+        for t in range(PACK - 1):
+            direct(t, 0, SHARE)
+            fetch(t, SHARE, S)
+            if t == 1:
+                place(0, SHARE, S)
+        last = PACK - 1
+        direct(last, 0, Q)
+        direct(last, Q, SHARE)
+        for lo, hi in PIECES:
+            fetch(last, lo, hi)
+        for lo, hi in PIECES:
+            place(last - 1, lo, hi)
 
         for lo, hi in UNITS:
             nc.vector.quantize_mx(

@@ -20,6 +20,7 @@ P = 128
 PACK = 4
 SHARE = 288
 Q = 128
+HELD = 320
 PIECES = ((SHARE, 384), (384, 512))
 UNITS = ((0, 128), (128, 256), (256, 384), (384, 512))
 
@@ -35,7 +36,7 @@ def tile_picked_rank_none_e_kernel(tc, xT, w1_words, w1_scales, offs, out):
         rows = keep.tile([P, PACK, S - SHARE], BF16, name="rows")
         w_codes = keep.tile([P, N], U32, name="w_codes", align_bytes=64)
         w_scales = keep.tile([P, N], U8, name="w_scales", align_bytes=64)
-        grouped = keep.tile([P, S, PACK], BF16, name="grouped", align_bytes=64)
+        grouped = keep.tile([P, HELD + S // 2, PACK], BF16, name="grouped", align_bytes=64)
         x_codes = keep.tile([P, S], U32, name="x_codes", align_bytes=64)
         x_scales = keep.tile([P, S], U8, name="x_scales", align_bytes=64)
 
@@ -89,29 +90,43 @@ def tile_picked_rank_none_e_kernel(tc, xT, w1_words, w1_scales, offs, out):
                 in_=grouped[:, lo:hi, :].rearrange("p c t -> p (c t)"),
             )
 
-        blocks = N // P
-        scores = [psum.tile([P, S], F32, name="scores%d" % b) for b in range(blocks)]
-        for b in range(blocks):
-            for lo, hi in UNITS if b == 0 else ((0, S),):
-                cols = slice(lo, hi)
-                nc.tensor.matmul_mx(
-                    out=scores[b][:, cols],
-                    lhsT=w_codes[:, b * P : (b + 1) * P].bitcast(FP8X4),
-                    lhsT_scale=w_scales[:, b * P : (b + 1) * P],
-                    rhs=x_codes[:, cols].bitcast(FP8X4),
-                    rhs_scale=x_scales[:, cols],
-                    start=True,
-                    stop=True,
-                )
+        def product(target, b, lo, hi):
+            nc.tensor.matmul_mx(
+                out=target,
+                lhsT=w_codes[:, b * P : (b + 1) * P].bitcast(FP8X4),
+                lhsT_scale=w_scales[:, b * P : (b + 1) * P],
+                rhs=x_codes[:, lo:hi].bitcast(FP8X4),
+                rhs_scale=x_scales[:, lo:hi],
+                start=True,
+                stop=True,
+            )
 
-        for b in range(blocks):
-            neg_max = keep.tile([P, 1], F32, name="neg_max%d" % b)
+        head = psum.tile([P, Q], F32, name="head")
+        rest = psum.tile([P, S - Q], F32, name="rest")
+        second = psum.tile([P, S], F32, name="second")
+        product(head[:], 0, 0, Q)
+        product(second[:, :Q], 1, 0, Q)
+        for lo, hi in UNITS[1:]:
+            product(rest[:, lo - Q : hi - Q], 0, lo, hi)
+        for lo, hi in ((Q, 2 * Q), (2 * Q, S)):
+            product(second[:, lo:hi], 1, lo, hi)
+
+        def finish(b, source, sign, neg_max):
             total = keep.tile([P, 1], F32, name="total%d" % b)
             inverse = keep.tile([P, 1], F32, name="inverse%d" % b)
             e = keep.tile([P, S], F32, name="e%d" % b)
-            nc.vector.tensor_reduce(neg_max[:], scores[b][:], AX.X, ALU.max, negate=True)
-            nc.scalar.activation(e[:], scores[b][:], ACT.Exp, bias=neg_max[:], scale=1.0, accum_out=total[:])
-            nc.vector.reciprocal(inverse[:], total[:])
             result = keep.tile([P, S], F32, name="result%d" % b)
+            nc.scalar.activation(e[:], source, ACT.Exp, bias=neg_max[:], scale=sign, accum_out=total[:])
+            nc.vector.reciprocal(inverse[:], total[:])
             nc.vector.tensor_scalar(result[:], e[:], inverse[:], None, ALU.mult)
             nc.sync.dma_start(out=out[b * P : (b + 1) * P, :], in_=result[:])
+
+        negated = grouped[:, HELD:, :].rearrange("p c t -> p (c t)").bitcast(F32)
+        neg_head = keep.tile([P, 1], F32, name="neg_head")
+        neg_max0 = keep.tile([P, 1], F32, name="neg_max0")
+        neg_max1 = keep.tile([P, 1], F32, name="neg_max1")
+        nc.vector.tensor_scalar(negated[:, :Q], head[:], -1.0, None, ALU.mult, ALU.min, accum_out=neg_head[:])
+        nc.vector.tensor_scalar(negated[:, Q:], rest[:], -1.0, neg_head[:], ALU.mult, ALU.min, accum_out=neg_max0[:])
+        nc.vector.tensor_reduce(neg_max1[:], second[:], AX.X, ALU.max, negate=True)
+        finish(0, negated, -1.0, neg_max0)
+        finish(1, second[:], 1.0, neg_max1)

@@ -21,7 +21,8 @@ PACK = 4
 SHARE = 288
 Q = 128
 HELD = 320
-PIECES = ((SHARE, 384), (384, 512))
+VECTOR_RUNS = ((0, 160), (256, 384))
+SCALAR_RUNS = ((160, 256), (384, 512))
 UNITS = ((0, 128), (128, 256), (256, 384), (384, 512))
 
 
@@ -33,11 +34,14 @@ def tile_picked_rank_none_e_kernel(tc, xT, w1_words, w1_scales, offs, out):
 
         offsets = keep.tile([P, S // 16], U16, name="offsets")
         raw = [keep.tile([P, T], F32, name="raw%d" % t) for t in range(PACK)]
-        rows = keep.tile([P, PACK, S - SHARE], BF16, name="rows")
+        early = keep.tile([P, 2, S - SHARE], BF16, name="early")
+        late = [
+            keep.tile([P, 2, hi - lo], BF16, name="late%d" % i, tag="late%d" % i, align_bytes=64)
+            for i, (lo, hi) in enumerate(SCALAR_RUNS)
+        ]
         w_codes = keep.tile([P, N], U32, name="w_codes", align_bytes=64)
         w_scales = keep.tile([P, N], U8, name="w_scales", align_bytes=64)
         grouped = keep.tile([P, HELD + S // 2, PACK], BF16, name="grouped", align_bytes=64)
-        x_codes = keep.tile([P, S], U32, name="x_codes", align_bytes=64)
         x_scales = keep.tile([P, S], U8, name="x_scales", align_bytes=64)
 
         planes = xT.rearrange("(p t) c -> p t c", t=PACK)
@@ -63,29 +67,36 @@ def tile_picked_rank_none_e_kernel(tc, xT, w1_words, w1_scales, offs, out):
         def direct(t, lo, hi):
             nc.vector.tensor_copy(grouped[:, lo:hi, t], raw[t][:].indirect(picks(lo, hi)))
 
-        def fetch(t, lo, hi):
-            nc.scalar.activation(rows[:, t, lo - SHARE : hi - SHARE], raw[t][:].indirect(picks(lo, hi)), ACT.Copy)
+        def fetch(rows, t, lo, hi):
+            nc.scalar.activation(rows[:, t % 2, :], raw[t][:].indirect(picks(lo, hi)), ACT.Copy)
 
-        def place(t, lo, hi):
-            pair = rows[:, t : t + 2, lo - SHARE : hi - SHARE].rearrange("p u c -> p c u")
-            nc.scalar.copy(grouped[:, lo:hi, t : t + 2], pair)
+        def place(rows, t, lo, hi):
+            nc.scalar.copy(grouped[:, lo:hi, t : t + 2], rows[:].rearrange("p u c -> p c u"))
 
-        for t in range(PACK - 1):
+        for t in (0, 1):
             direct(t, 0, SHARE)
-            fetch(t, SHARE, S)
-            if t == 1:
-                place(0, SHARE, S)
-        last = PACK - 1
-        direct(last, 0, Q)
-        direct(last, Q, SHARE)
-        for lo, hi in PIECES:
-            fetch(last, lo, hi)
-        for lo, hi in PIECES:
-            place(last - 1, lo, hi)
+            fetch(early, t, SHARE, S)
+        place(early, 0, SHARE, S)
+        for t in (2, 3):
+            for lo, hi in VECTOR_RUNS:
+                direct(t, lo, hi)
+            for rows, (lo, hi) in zip(late, SCALAR_RUNS):
+                fetch(rows, t, lo, hi)
+        for rows, (lo, hi) in zip(late, SCALAR_RUNS):
+            place(rows, 2, lo, hi)
+
+        half = S // 2
+        x_codes = [
+            keep.tile([P, half], U32, name="x_codes0", align_bytes=64),
+            keep.tile([P, half], U32, name="x_codes1", tag="late0", align_bytes=64),
+        ]
+
+        def codes(lo, hi):
+            return x_codes[lo // half][:, lo % half : lo % half + hi - lo].bitcast(FP8X4)
 
         for lo, hi in UNITS:
             nc.vector.quantize_mx(
-                out=x_codes[:, lo:hi].bitcast(FP8X4),
+                out=codes(lo, hi),
                 scales=x_scales[:, lo:hi],
                 in_=grouped[:, lo:hi, :].rearrange("p c t -> p (c t)"),
             )
@@ -95,7 +106,7 @@ def tile_picked_rank_none_e_kernel(tc, xT, w1_words, w1_scales, offs, out):
                 out=target,
                 lhsT=w_codes[:, b * P : (b + 1) * P].bitcast(FP8X4),
                 lhsT_scale=w_scales[:, b * P : (b + 1) * P],
-                rhs=x_codes[:, lo:hi].bitcast(FP8X4),
+                rhs=codes(lo, hi),
                 rhs_scale=x_scales[:, lo:hi],
                 start=True,
                 stop=True,

@@ -85,14 +85,12 @@ def tile_picked_rank_none_e_kernel(tc, xT, w1_words, w1_scales, offs, out):
         for rows, (lo, hi) in zip(late, SCALAR_RUNS):
             place(rows, 2, lo, hi)
 
-        half = S // 2
-        x_codes = [
-            keep.tile([P, half], U32, name="x_codes0", align_bytes=64),
-            keep.tile([P, half], U32, name="x_codes1", tag="late0", align_bytes=64),
-        ]
+        head_codes = keep.tile([P, Q], U32, name="head_codes", align_bytes=64)
+        rest_codes = keep.tile([P, S - Q], U32, name="rest_codes", tag="late0", align_bytes=64)
 
         def codes(lo, hi):
-            return x_codes[lo // half][:, lo % half : lo % half + hi - lo].bitcast(FP8X4)
+            tile = head_codes[:, lo:hi] if hi <= Q else rest_codes[:, lo - Q : hi - Q]
+            return tile.bitcast(FP8X4)
 
         for lo, hi in UNITS:
             nc.vector.quantize_mx(
@@ -117,9 +115,9 @@ def tile_picked_rank_none_e_kernel(tc, xT, w1_words, w1_scales, offs, out):
         second = psum.tile([P, S], F32, name="second")
         product(head[:], 0, 0, Q)
         product(second[:, :Q], 1, 0, Q)
-        for lo, hi in UNITS[1:]:
+        for lo, hi in ((Q, S - Q), (S - Q, S)):
             product(rest[:, lo - Q : hi - Q], 0, lo, hi)
-        for lo, hi in ((Q, 2 * Q), (2 * Q, S)):
+        for lo, hi in ((S - Q, S), (Q, S - Q)):
             product(second[:, lo:hi], 1, lo, hi)
 
         def finish(b, source, sign, neg_max):

@@ -52,14 +52,15 @@ def tile_picked_rank_none_e_kernel(tc, xT, w1_words, w1_scales, offs, out):
         nc.scalar.activation(warm_out[:], warm_in[:], ACT.Exp)
         nc.sync.dma_start(out=raw[0][:], in_=planes[:, 0, :])
         nc.sync.dma_start(offsets[:], offs)
-        for t in range(1, PACK):
-            nc.sync.dma_start(out=raw[t][:], in_=planes[:, t, :])
-        nc.sync.dma_start(out=w_codes[:].bitcast(I32), in_=w1_words[0].rearrange("p n r -> p (n r)").bitcast(I32))
+        nc.sync.dma_start(out=raw[1][:], in_=planes[:, 1, :])
         for q in range(4):
-            nc.scalar.dma_start(
+            nc.sync.dma_start(
                 out=w_scales[32 * q : 32 * q + 4, :].bitcast(I32),
                 in_=w1_scales[0, 4 * q : 4 * q + 4, :].bitcast(I32),
             )
+        for t in (2, 3):
+            nc.sync.dma_start(out=raw[t][:], in_=planes[:, t, :])
+        nc.sync.dma_start(out=w_codes[:].bitcast(I32), in_=w1_words[0].rearrange("p n r -> p (n r)").bitcast(I32))
 
         def picks(lo, hi):
             return offsets[:, lo // 16 : hi // 16]

@@ -33,13 +33,13 @@ def tile_picked_rank_none_e_kernel(tc, xT, w1_words, w1_scales, offs, out):
         psum = ctx.enter_context(tc.psum_pool(name="psum", bufs=1))
 
         offsets = keep.tile([P, S // 16], U16, name="offsets")
-        raw = [keep.tile([P, T], F32, name="raw%d" % t) for t in range(PACK)]
+        raw = [keep.tile([P, T], F32, name="raw%d" % t, align_bytes=256) for t in range(PACK)]
         early = keep.tile([P, 2, S - SHARE], BF16, name="early")
         late = [
             keep.tile([P, 2, hi - lo], BF16, name="late%d" % i, tag="late%d" % i, align_bytes=64)
             for i, (lo, hi) in enumerate(SCALAR_RUNS)
         ]
-        w_codes = keep.tile([P, N], U32, name="w_codes", align_bytes=64)
+        w_codes = keep.tile([P, N], U32, name="w_codes", align_bytes=256)
         w_scales = keep.tile([P, N], U8, name="w_scales", align_bytes=64)
         grouped = keep.tile([P, HELD + S // 2, PACK], BF16, name="grouped", align_bytes=64)
         x_scales = keep.tile([P, S], U8, name="x_scales", align_bytes=64)
@@ -125,7 +125,7 @@ def tile_picked_rank_none_e_kernel(tc, xT, w1_words, w1_scales, offs, out):
             total = keep.tile([P, 1], F32, name="total%d" % b)
             inverse = keep.tile([P, 1], F32, name="inverse%d" % b)
             e = keep.tile([P, S], F32, name="e%d" % b)
-            result = keep.tile([P, S], F32, name="result%d" % b)
+            result = keep.tile([P, S], F32, name="result%d" % b, align_bytes=256)
             nc.scalar.activation(e[:], source, ACT.Exp, bias=neg_max[:], scale=sign, accum_out=total[:])
             nc.vector.reciprocal(inverse[:], total[:])
             nc.vector.tensor_scalar(result[:], e[:], inverse[:], None, ALU.mult)

@@ -21,6 +21,7 @@ PACK = 4
 SHARE = 288
 Q = 128
 HELD = 320
+EARLY_RUNS = ((SHARE, 384), (384, 512))
 VECTOR_RUNS = ((0, 160), (256, 384))
 SCALAR_RUNS = ((160, 256), (384, 512))
 UNITS = ((0, 128), (128, 256), (256, 384), (384, 512))
@@ -34,7 +35,7 @@ def tile_picked_rank_none_e_kernel(tc, xT, w1_words, w1_scales, offs, out):
 
         offsets = keep.tile([P, S // 16], U16, name="offsets")
         raw = [keep.tile([P, T], F32, name="raw%d" % t, align_bytes=256) for t in range(PACK)]
-        early = keep.tile([P, 2, S - SHARE], BF16, name="early")
+        early = [keep.tile([P, 2, hi - lo], BF16, name="early%d" % i) for i, (lo, hi) in enumerate(EARLY_RUNS)]
         late = [
             keep.tile([P, 2, hi - lo], BF16, name="late%d" % i, tag="late%d" % i, align_bytes=64)
             for i, (lo, hi) in enumerate(SCALAR_RUNS)
@@ -76,8 +77,10 @@ def tile_picked_rank_none_e_kernel(tc, xT, w1_words, w1_scales, offs, out):
 
         for t in (0, 1):
             direct(t, 0, SHARE)
-            fetch(early, t, SHARE, S)
-        place(early, 0, SHARE, S)
+            for rows, (lo, hi) in zip(early, EARLY_RUNS):
+                fetch(rows, t, lo, hi)
+        for rows, (lo, hi) in zip(early, EARLY_RUNS):
+            place(rows, 0, lo, hi)
         for t in (2, 3):
             for lo, hi in VECTOR_RUNS:
                 direct(t, lo, hi)

@@ -124,15 +124,17 @@ def tile_picked_rank_none_e_kernel(tc, xT, w1_words, w1_scales, offs, out):
         for lo, hi in ((S - Q, S), (Q, S - Q)):
             product(second[:, lo:hi], 1, lo, hi)
 
-        def finish(b, source, sign, neg_max):
+        def finish(b, source, sign, neg_max, width):
             total = keep.tile([P, 1], F32, name="total%d" % b)
             inverse = keep.tile([P, 1], F32, name="inverse%d" % b)
             e = keep.tile([P, S], F32, name="e%d" % b)
             result = keep.tile([P, S], F32, name="result%d" % b, align_bytes=256)
             nc.scalar.activation(e[:], source, ACT.Exp, bias=neg_max[:], scale=sign, accum_out=total[:])
             nc.vector.reciprocal(inverse[:], total[:])
-            nc.vector.tensor_scalar(result[:], e[:], inverse[:], None, ALU.mult)
-            nc.sync.dma_start(out=out[b * P : (b + 1) * P, :], in_=result[:])
+            for lo in range(0, S, width):
+                cols = slice(lo, lo + width)
+                nc.vector.tensor_scalar(result[:, cols], e[:, cols], inverse[:], None, ALU.mult)
+                nc.sync.dma_start(out=out[b * P : (b + 1) * P, cols], in_=result[:, cols])
 
         negated = grouped[:, HELD:, :].rearrange("p c t -> p (c t)").bitcast(F32)
         neg_head = keep.tile([P, 1], F32, name="neg_head")
@@ -141,5 +143,5 @@ def tile_picked_rank_none_e_kernel(tc, xT, w1_words, w1_scales, offs, out):
         nc.vector.tensor_scalar(negated[:, :Q], head[:], -1.0, None, ALU.mult, ALU.min, accum_out=neg_head[:])
         nc.vector.tensor_scalar(negated[:, Q:], rest[:], -1.0, neg_head[:], ALU.mult, ALU.min, accum_out=neg_max0[:])
         nc.vector.tensor_reduce(neg_max1[:], second[:], AX.X, ALU.max, negate=True)
-        finish(0, negated, -1.0, neg_max0)
-        finish(1, second[:], 1.0, neg_max1)
+        finish(0, negated, -1.0, neg_max0, S // 2)
+        finish(1, second[:], 1.0, neg_max1, S // 2)

@@ -21,6 +21,7 @@ PACK = 4
 SHARE = 288
 Q = 128
 HELD = 320
+FIRST = 192
 EARLY_RUNS = ((SHARE, 384), (384, 512))
 VECTOR_RUNS = ((0, 160), (256, 384))
 SCALAR_RUNS = ((160, 256), (384, 512))
@@ -124,15 +125,14 @@ def tile_picked_rank_none_e_kernel(tc, xT, w1_words, w1_scales, offs, out):
         for lo, hi in ((S - Q, S), (Q, S - Q)):
             product(second[:, lo:hi], 1, lo, hi)
 
-        def finish(b, source, sign, neg_max, width):
+        def finish(b, source, sign, neg_max):
             total = keep.tile([P, 1], F32, name="total%d" % b)
             inverse = keep.tile([P, 1], F32, name="inverse%d" % b)
             e = keep.tile([P, S], F32, name="e%d" % b)
             result = keep.tile([P, S], F32, name="result%d" % b, align_bytes=256)
             nc.scalar.activation(e[:], source, ACT.Exp, bias=neg_max[:], scale=sign, accum_out=total[:])
             nc.vector.reciprocal(inverse[:], total[:])
-            for lo in range(0, S, width):
-                cols = slice(lo, lo + width)
+            for cols in (slice(0, FIRST), slice(FIRST, S)):
                 nc.vector.tensor_scalar(result[:, cols], e[:, cols], inverse[:], None, ALU.mult)
                 nc.sync.dma_start(out=out[b * P : (b + 1) * P, cols], in_=result[:, cols])
 
@@ -143,5 +143,5 @@ def tile_picked_rank_none_e_kernel(tc, xT, w1_words, w1_scales, offs, out):
         nc.vector.tensor_scalar(negated[:, :Q], head[:], -1.0, None, ALU.mult, ALU.min, accum_out=neg_head[:])
         nc.vector.tensor_scalar(negated[:, Q:], rest[:], -1.0, neg_head[:], ALU.mult, ALU.min, accum_out=neg_max0[:])
         nc.vector.tensor_reduce(neg_max1[:], second[:], AX.X, ALU.max, negate=True)
-        finish(0, negated, -1.0, neg_max0, S // 2)
-        finish(1, second[:], 1.0, neg_max1, S // 2)
+        finish(0, negated, -1.0, neg_max0)
+        finish(1, second[:], 1.0, neg_max1)

@@ -18,13 +18,13 @@ AX = mybir.AxisListType
 
 P = 128
 PACK = 4
-SHARE = 288
 Q = 128
 HELD = 320
 FIRST = 192
-EARLY_RUNS = ((SHARE, 384), (384, 512))
-VECTOR_RUNS = ((0, 160), (256, 384))
-SCALAR_RUNS = ((160, 256), (384, 512))
+LOW_VECTOR = ((0, 256),)
+LOW_SCALAR = ((256, 512),)
+HIGH_VECTOR = ((128, 352),)
+HIGH_SCALAR = ((0, 128), (352, 416), (416, 512))
 UNITS = ((0, 128), (128, 256), (256, 384), (384, 512))
 
 
@@ -36,15 +36,11 @@ def tile_picked_rank_none_e_kernel(tc, xT, w1_words, w1_scales, offs, out):
 
         offsets = keep.tile([P, S // 16], U16, name="offsets")
         raw = [keep.tile([P, T], F32, name="raw%d" % t, align_bytes=256) for t in range(PACK)]
-        early = [keep.tile([P, 2, hi - lo], BF16, name="early%d" % i) for i, (lo, hi) in enumerate(EARLY_RUNS)]
-        late = [
-            keep.tile([P, 2, hi - lo], BF16, name="late%d" % i, tag="late%d" % i, align_bytes=64)
-            for i, (lo, hi) in enumerate(SCALAR_RUNS)
-        ]
         w_codes = keep.tile([P, N], U32, name="w_codes", align_bytes=256)
         w_scales = keep.tile([P, N], U8, name="w_scales", align_bytes=64)
         grouped = keep.tile([P, HELD + S // 2, PACK], BF16, name="grouped", align_bytes=64)
         x_scales = keep.tile([P, S], U8, name="x_scales", align_bytes=64)
+        x_codes = keep.tile([P, S], U32, name="x_codes", align_bytes=64)
 
         planes = xT.rearrange("(p t) c -> p t c", t=PACK)
         nc.vector.memset(w_scales[:].bitcast(I32), 0)
@@ -52,54 +48,30 @@ def tile_picked_rank_none_e_kernel(tc, xT, w1_words, w1_scales, offs, out):
         warm_out = keep.tile([P, 1], F32, name="warm_out")
         nc.vector.memset(warm_in[:], 0.0)
         nc.scalar.activation(warm_out[:], warm_in[:], ACT.Exp)
-        nc.sync.dma_start(out=raw[0][:], in_=planes[:, 0, :])
+        nc.sync.dma_start(out=raw[2][:], in_=planes[:, 2, :])
         nc.sync.dma_start(offsets[:], offs)
-        nc.sync.dma_start(out=raw[1][:], in_=planes[:, 1, :])
+        nc.sync.dma_start(out=raw[0][:], in_=planes[:, 0, :])
         for q in range(4):
             nc.sync.dma_start(
                 out=w_scales[32 * q : 32 * q + 4, :].bitcast(I32),
                 in_=w1_scales[0, 4 * q : 4 * q + 4, :].bitcast(I32),
             )
-        for t in (2, 3):
+        for t in (1, 3):
             nc.sync.dma_start(out=raw[t][:], in_=planes[:, t, :])
         nc.sync.dma_start(out=w_codes[:].bitcast(I32), in_=w1_words[0].rearrange("p n r -> p (n r)").bitcast(I32))
 
-        def picks(lo, hi):
-            return offsets[:, lo // 16 : hi // 16]
+        def picked(t, lo, hi):
+            return raw[t][:].indirect(offsets[:, lo // 16 : hi // 16])
 
-        def direct(t, lo, hi):
-            nc.vector.tensor_copy(grouped[:, lo:hi, t], raw[t][:].indirect(picks(lo, hi)))
-
-        def fetch(rows, t, lo, hi):
-            nc.scalar.activation(rows[:, t % 2, :], raw[t][:].indirect(picks(lo, hi)), ACT.Copy)
-
-        def place(rows, t, lo, hi):
-            nc.scalar.copy(grouped[:, lo:hi, t : t + 2], rows[:].rearrange("p u c -> p c u"))
-
-        for t in (0, 1):
-            direct(t, 0, SHARE)
-            for rows, (lo, hi) in zip(early, EARLY_RUNS):
-                fetch(rows, t, lo, hi)
-        for rows, (lo, hi) in zip(early, EARLY_RUNS):
-            place(rows, 0, lo, hi)
-        for t in (2, 3):
-            for lo, hi in VECTOR_RUNS:
-                direct(t, lo, hi)
-            for rows, (lo, hi) in zip(late, SCALAR_RUNS):
-                fetch(rows, t, lo, hi)
-        for rows, (lo, hi) in zip(late, SCALAR_RUNS):
-            place(rows, 2, lo, hi)
-
-        head_codes = keep.tile([P, Q], U32, name="head_codes", align_bytes=64)
-        rest_codes = keep.tile([P, S - Q], U32, name="rest_codes", tag="late0", align_bytes=64)
-
-        def codes(lo, hi):
-            tile = head_codes[:, lo:hi] if hi <= Q else rest_codes[:, lo - Q : hi - Q]
-            return tile.bitcast(FP8X4)
+        for t in (2, 0, 1, 3):
+            for lo, hi in HIGH_VECTOR if t >= 2 else LOW_VECTOR:
+                nc.vector.tensor_copy(grouped[:, lo:hi, t], picked(t, lo, hi))
+            for lo, hi in HIGH_SCALAR if t >= 2 else LOW_SCALAR:
+                nc.scalar.activation(grouped[:, lo:hi, t], picked(t, lo, hi), ACT.Copy)
 
         for lo, hi in UNITS:
             nc.vector.quantize_mx(
-                out=codes(lo, hi),
+                out=x_codes[:, lo:hi].bitcast(FP8X4),
                 scales=x_scales[:, lo:hi],
                 in_=grouped[:, lo:hi, :].rearrange("p c t -> p (c t)"),
             )
@@ -109,7 +81,7 @@ def tile_picked_rank_none_e_kernel(tc, xT, w1_words, w1_scales, offs, out):
                 out=target,
                 lhsT=w_codes[:, b * P : (b + 1) * P].bitcast(FP8X4),
                 lhsT_scale=w_scales[:, b * P : (b + 1) * P],
-                rhs=codes(lo, hi),
+                rhs=x_codes[:, lo:hi].bitcast(FP8X4),
                 rhs_scale=x_scales[:, lo:hi],
                 start=True,
                 stop=True,

@@ -23,8 +23,8 @@ HELD = 320
 FIRST = 192
 LOW_VECTOR = ((0, 256),)
 LOW_SCALAR = ((256, 512),)
-HIGH_VECTOR = ((128, 352),)
-HIGH_SCALAR = ((0, 128), (352, 416), (416, 512))
+HIGH_VECTOR = ((0, 128), (256, 384))
+HIGH_SCALAR = ((128, 256), (384, 512))
 UNITS = ((0, 128), (128, 256), (256, 384), (384, 512))
 
 

@@ -91,11 +91,9 @@ def tile_picked_rank_none_e_kernel(tc, xT, w1_words, w1_scales, offs, out):
         rest = psum.tile([P, S - Q], F32, name="rest")
         second = psum.tile([P, S], F32, name="second")
         product(head[:], 0, 0, Q)
-        product(second[:, :Q], 1, 0, Q)
-        for lo, hi in ((Q, S - Q), (S - Q, S)):
+        for lo, hi in UNITS[1:]:
             product(rest[:, lo - Q : hi - Q], 0, lo, hi)
-        for lo, hi in ((S - Q, S), (Q, S - Q)):
-            product(second[:, lo:hi], 1, lo, hi)
+        product(second[:], 1, 0, S)
 
         def finish(b, source, sign, neg_max):
             total = keep.tile([P, 1], F32, name="total%d" % b)

from contextlib import ExitStack

import concourse.mybir as mybir

K, T, S, N = 512, 1024, 512, 256
FLOPS = 2 * K * S * N

F32 = mybir.dt.float32
BF16 = mybir.dt.bfloat16
I32 = mybir.dt.int32
U32 = mybir.dt.uint32
U16 = mybir.dt.uint16
U8 = mybir.dt.uint8
FP8X4 = mybir.dt.float8_e4m3fn_x4
ACT = mybir.ActivationFunctionType
ALU = mybir.AluOpType
AX = mybir.AxisListType

P = 128
PACK = 4
Q = 128
HELD = 320
FIRST = 192
LOW_VECTOR = ((0, 256),)
LOW_SCALAR = ((256, 512),)
HIGH_VECTOR = ((0, 128), (256, 384))
HIGH_SCALAR = ((128, 256), (384, 512))
UNITS = ((0, 128), (128, 256), (256, 384), (384, 512))


def tile_picked_rank_none_e_kernel(tc, xT, w1_words, w1_scales, offs, out):
    nc = tc.nc
    with ExitStack() as ctx:
        keep = ctx.enter_context(tc.tile_pool(name="keep", bufs=1))
        psum = ctx.enter_context(tc.psum_pool(name="psum", bufs=1))

        offsets = keep.tile([P, S // 16], U16, name="offsets")
        raw = [keep.tile([P, T], F32, name="raw%d" % t, align_bytes=256) for t in range(PACK)]
        w_codes = keep.tile([P, N], U32, name="w_codes", align_bytes=256)
        w_scales = keep.tile([P, N], U8, name="w_scales", align_bytes=64)
        grouped = keep.tile([P, HELD + S // 2, PACK], BF16, name="grouped", align_bytes=64)
        x_scales = keep.tile([P, S], U8, name="x_scales", align_bytes=64)
        x_codes = keep.tile([P, S], U32, name="x_codes", align_bytes=64)

        planes = xT.rearrange("(p t) c -> p t c", t=PACK)
        nc.vector.memset(w_scales[:].bitcast(I32), 0)
        warm_in = keep.tile([P, 1], F32, name="warm_in")
        warm_out = keep.tile([P, 1], F32, name="warm_out")
        nc.vector.memset(warm_in[:], 0.0)
        nc.scalar.activation(warm_out[:], warm_in[:], ACT.Exp)
        nc.sync.dma_start(out=raw[2][:], in_=planes[:, 2, :])
        nc.sync.dma_start(offsets[:], offs)
        nc.sync.dma_start(out=raw[0][:], in_=planes[:, 0, :])
        for q in range(4):
            nc.sync.dma_start(
                out=w_scales[32 * q : 32 * q + 4, :].bitcast(I32),
                in_=w1_scales[0, 4 * q : 4 * q + 4, :].bitcast(I32),
            )
        for t in (1, 3):
            nc.sync.dma_start(out=raw[t][:], in_=planes[:, t, :])
        nc.sync.dma_start(out=w_codes[:].bitcast(I32), in_=w1_words[0].rearrange("p n r -> p (n r)").bitcast(I32))

        def picked(t, lo, hi):
            return raw[t][:].indirect(offsets[:, lo // 16 : hi // 16])

        for t in (2, 0, 1, 3):
            for lo, hi in HIGH_VECTOR if t >= 2 else LOW_VECTOR:
                nc.vector.tensor_copy(grouped[:, lo:hi, t], picked(t, lo, hi))
            for lo, hi in HIGH_SCALAR if t >= 2 else LOW_SCALAR:
                nc.scalar.activation(grouped[:, lo:hi, t], picked(t, lo, hi), ACT.Copy)

        for lo, hi in UNITS:
            nc.vector.quantize_mx(
                out=x_codes[:, lo:hi].bitcast(FP8X4),
                scales=x_scales[:, lo:hi],
                in_=grouped[:, lo:hi, :].rearrange("p c t -> p (c t)"),
            )

        def product(target, b, lo, hi):
            nc.tensor.matmul_mx(
                out=target,
                lhsT=w_codes[:, b * P : (b + 1) * P].bitcast(FP8X4),
                lhsT_scale=w_scales[:, b * P : (b + 1) * P],
                rhs=x_codes[:, lo:hi].bitcast(FP8X4),
                rhs_scale=x_scales[:, lo:hi],
                start=True,
                stop=True,
            )

        head = psum.tile([P, Q], F32, name="head")
        rest = psum.tile([P, S - Q], F32, name="rest")
        second = psum.tile([P, S], F32, name="second")
        product(head[:], 0, 0, Q)
        for lo, hi in UNITS[1:]:
            product(rest[:, lo - Q : hi - Q], 0, lo, hi)
        product(second[:], 1, 0, S)

        def finish(b, source, sign, neg_max):
            total = keep.tile([P, 1], F32, name="total%d" % b)
            inverse = keep.tile([P, 1], F32, name="inverse%d" % b)
            e = keep.tile([P, S], F32, name="e%d" % b)
            result = keep.tile([P, S], F32, name="result%d" % b, align_bytes=256)
            nc.scalar.activation(e[:], source, ACT.Exp, bias=neg_max[:], scale=sign, accum_out=total[:])
            nc.vector.reciprocal(inverse[:], total[:])
            for cols in (slice(0, FIRST), slice(FIRST, S)):
                nc.vector.tensor_scalar(result[:, cols], e[:, cols], inverse[:], None, ALU.mult)
                nc.sync.dma_start(out=out[b * P : (b + 1) * P, cols], in_=result[:, cols])

        negated = grouped[:, HELD:, :].rearrange("p c t -> p (c t)").bitcast(F32)
        neg_head = keep.tile([P, 1], F32, name="neg_head")
        neg_max0 = keep.tile([P, 1], F32, name="neg_max0")
        neg_max1 = keep.tile([P, 1], F32, name="neg_max1")
        nc.vector.tensor_scalar(negated[:, :Q], head[:], -1.0, None, ALU.mult, ALU.min, accum_out=neg_head[:])
        nc.vector.tensor_scalar(negated[:, Q:], rest[:], -1.0, neg_head[:], ALU.mult, ALU.min, accum_out=neg_max0[:])
        nc.vector.tensor_reduce(neg_max1[:], second[:], AX.X, ALU.max, negate=True)
        finish(0, negated, -1.0, neg_max0)
        finish(1, second[:], 1.0, neg_max1)
